import numpy as np
import ml_dtypes


def mxq(x, axis, fmt="e4m3"):
    dtype, down = {"e4m3": (ml_dtypes.float8_e4m3fn, 7), "e5m2": (ml_dtypes.float8_e5m2, 14)}[fmt]
    v = np.moveaxis(np.asarray(x, np.float32).astype(ml_dtypes.bfloat16).astype(np.float64), axis, -1)
    blocks = v.reshape(v.shape[:-1] + (-1, 32))
    amax = np.abs(blocks).max(-1, keepdims=True)
    byte = np.maximum(np.where(amax > 0, np.frexp(amax)[1] - 1 + 127, 0) - down, 1)
    scale = np.exp2(byte - 127.0)
    codes = (blocks / scale).astype(np.float32).astype(dtype).astype(np.float64)
    return np.moveaxis((codes * scale).reshape(v.shape), -1, axis)


WIDE = False


def mx_kscale(k):
    if not WIDE:
        return np.ones(k)
    levels = np.array([10, -10, 5, -5, 0])
    if k % 512:
        return np.exp2(np.random.permutation(np.resize(levels, k // 32))).repeat(32)
    a = np.empty((k // 512, 16))
    for p in range(k // 512):
        a[p, :8] = np.random.permutation(np.resize(levels, 8))
        for g in range(8):
            far = levels[np.abs(levels - a[p, g]) >= 10]
            a[p, g + 8] = far[np.random.randint(len(far))]
    return np.exp2(a.ravel()).repeat(32)


BF16 = ml_dtypes.bfloat16


def bf(x):
    return np.asarray(x, np.float32).astype(BF16)


def f64(x):
    return np.asarray(x).astype(np.float64)


E2M1 = np.array([0.0, 0.5, 1.0, 1.5, 2.0, 3.0, 4.0, 6.0, -0.0, -0.5, -1.0, -1.5, -2.0, -3.0, -4.0, -6.0])


def pack_weight(w, fmt):
    k, n = w.shape
    w = f64(bf(w)).reshape(k // 32, 32, n)
    amax = np.abs(w).max(1)
    if fmt == "e4m3":
        byte = np.frexp(amax)[1] - 1 + 127 - 7
    else:
        mant, ex = np.frexp(amax / 6.0)
        byte = np.where(mant > 0.5, ex, ex - 1) + 127
    byte = np.clip(np.where(amax > 0, byte, 1), 1, 254)
    scaled = (w * np.exp2(127.0 - byte)[:, None, :]).reshape(k, n).astype(np.float32)
    by_word = np.ascontiguousarray(scaled.reshape(k // 512, 128, 4, n).transpose(0, 1, 3, 2))
    if fmt == "e4m3":
        words = by_word.astype(ml_dtypes.float8_e4m3fn).view(np.uint8)
    else:
        c = by_word.astype(ml_dtypes.float4_e2m1fn).view(np.uint8) & 0xF
        words = c[..., 0::2] | (c[..., 1::2] << 4)
    return np.ascontiguousarray(words), np.ascontiguousarray(byte.astype(np.uint8).reshape(k // 512, 16, n))


def unpack_weight(words, scales, fmt):
    g, p, n, _ = words.shape
    if fmt == "e4m3":
        vals = np.ascontiguousarray(words).view(ml_dtypes.float8_e4m3fn).astype(np.float64)
    else:
        nib = np.empty((g, p, n, 4), np.uint8)
        nib[..., 0::2] = words & 0xF
        nib[..., 1::2] = words >> 4
        vals = E2M1[nib]
    vals = vals * np.repeat(np.exp2(scales.astype(np.float64) - 127.0), 8, axis=1)[..., None]
    return vals.transpose(0, 1, 3, 2).reshape(g * 512, n)
def pack4(w):
    words, scales = pack_weight(w, "e2m1")
    return words.reshape(words.shape[0], 128, -1), scales


def unpack4(words, scales):
    return unpack_weight(words.reshape(words.shape[0], 128, -1, 2), scales, "e2m1")


L, F, P, R = 1024, 512, 2048, 1024


def setup_inputs():
    s, t = mx_kscale(F), mx_kscale(L)
    spectra = np.random.standard_normal((L, F)) ** 2 * s
    abundance = np.exp(1.7 * np.random.standard_normal((F, P))) / (4 * F) / s[:, None]
    library = np.random.standard_normal((L, R)) ** 2 / np.sqrt(3 * L) / t[:, None]
    lib_words, lib_scales = pack4(library)
    return {"pixels": bf(np.random.standard_normal((L, P)) * t[:, None]),
            "spectra": bf(spectra),
            "abundance": bf(abundance),
            "read_var": bf(0.5 * np.exp(0.2 * np.random.standard_normal(L))),
            "lib_words": lib_words,
            "lib_scales": lib_scales}


def reference(pixels, spectra, abundance, read_var, lib_words, lib_scales):
    mu = mxq(f64(spectra), 1, "e4m3") @ mxq(f64(abundance), 0, "e4m3")
    var = mu + f64(read_var)[:, None]
    z = f64(pixels) / var
    lib = unpack4(lib_words, lib_scales)
    return lib.T @ mxq(z, 0, "e4m3")

@@ -1,0 +1,328 @@
+from contextlib import ExitStack
+
+import concourse.mybir as mybir
+from concourse.masks import make_identity
+
+L, F, P, R = 1024, 512, 2048, 1024
+FLOPS = 2 * L * F * P + 2 * L * R * P
+
+F32 = mybir.dt.float32
+BF16 = mybir.dt.bfloat16
+U32 = mybir.dt.uint32
+I32 = mybir.dt.int32
+U8 = mybir.dt.uint8
+FP8X4 = mybir.dt.float8_e4m3fn_x4
+FP4X4 = mybir.dt.float4_e2m1fn_x4
+ACT = mybir.ActivationFunctionType
+ALU = mybir.AluOpType
+
+PARTS = 128
+GROUPS = L // 512
+WIDTHS = (256, 512, 512, 512, 256)
+STARTS = tuple(sum(WIDTHS[:i]) for i in range(len(WIDTHS)))
+TILES = len(WIDTHS)
+UNITS = TILES * GROUPS
+WMAX = 512
+
+
+def tile_poisson_weighted_library_correlation_s13_kernel(
+    tc, pixels, spectra, abundance, read_var, lib_words, lib_scales, out
+):
+    nc = tc.nc
+    with ExitStack() as ctx:
+        keep = ctx.enter_context(tc.tile_pool(name="keep", bufs=1))
+        work = ctx.enter_context(tc.tile_pool(name="work", bufs=3))
+        psum = ctx.enter_context(tc.psum_pool(name="psum", bufs=1))
+        ctx.enter_context(tc.manual_schedule())
+
+        spec_v = spectra.rearrange("(g m t) k -> g m t k", m=128, t=4)
+        ab_v = abundance.rearrange("(p j) n -> p j n", j=4)
+        px_v = pixels.rearrange("(g p t) n -> g p t n", p=128, t=4)
+        rv_v = read_var.rearrange("(g p t) -> p g t", p=128, t=4)
+        words_v = lib_words.bitcast(I32)
+        scales_v = lib_scales.bitcast(I32).rearrange("g r n -> r g n")
+
+        warm = keep.tile([PARTS, 1], F32, name="warm")
+        nc.vector.memset(warm[:], 1.0)
+        ident = keep.tile([PARTS, PARTS], F32, name="ident")
+        make_identity(nc, ident[:])
+        plane = keep.tile([PARTS, GROUPS, R], U8, name="plane", align_bytes=64)
+        plane_words = plane[:].rearrange("p g n -> p (g n)").bitcast(I32)
+        nc.vector.memset(plane_words, 0)
+
+        rv16 = keep.tile([PARTS, GROUPS, 4], BF16, name="rv16")
+        with nc.allow_non_contiguous_dma(reason="2 KiB vector onto the partitions"):
+            nc.scalar.dma_start(out=rv16[:], in_=rv_v)
+        warm_out = keep.tile([PARTS, 1], F32, name="warm_out")
+        nc.scalar.activation(out=warm_out[:], in_=warm[:], func=ACT.Abs_reciprocal_sqrt)
+
+        sp_raw, ab_raw, px, lib = {}, {}, {}, []
+
+        def load_spec(g, h):
+            tl = keep.tile([PARTS, 2, F], BF16, name=f"sp_raw{g}{h}", align_bytes=64)
+            nc.sync.dma_start(out=tl[:], in_=spec_v[g, :, 2 * h : 2 * h + 2, :])
+            sp_raw[g, h] = tl
+
+        def load_ab(i, n):
+            w = sum(WIDTHS[i : i + n])
+            s = STARTS[i]
+            tl = keep.tile([PARTS, 4, w], BF16, name=f"ab_raw{i}", align_bytes=64)
+            nc.sync.dma_start(out=tl[:], in_=ab_v[:, :, s : s + w])
+            for k in range(i, i + n):
+                ab_raw[k] = tl[:, :, STARTS[k] - s : STARTS[k] - s + WIDTHS[k]]
+
+        def load_px(i, n, g):
+            w = sum(WIDTHS[i : i + n])
+            s = STARTS[i]
+            tl = keep.tile([PARTS, 4, w], BF16, name=f"px{i}{g}", align_bytes=64)
+            nc.sync.dma_start(out=tl[:], in_=px_v[g, :, :, s : s + w])
+            for k in range(i, i + n):
+                px[k, g] = tl[:, :, STARTS[k] - s : STARTS[k] - s + WIDTHS[k]]
+
+        def load_scales():
+            for q in range(4):
+                nc.sync.dma_start(
+                    out=plane_words[32 * q : 32 * q + 4, :].rearrange("p (g n) -> p g n", g=GROUPS),
+                    in_=scales_v[4 * q : 4 * q + 4],
+                )
+
+        def load_lib(g):
+            tl = keep.tile([PARTS, 2 * R], U8, name=f"lib{g}", align_bytes=64)
+            nc.sync.dma_start(out=tl[:].bitcast(I32), in_=words_v[g])
+            lib.append(tl)
+
+        load_spec(0, 0)
+        load_ab(0, 1)
+        load_spec(0, 1)
+        load_spec(1, 0)
+        load_spec(1, 1)
+        load_ab(1, 1)
+        load_px(0, 2, 0)
+        load_px(0, 2, 1)
+        load_ab(2, 3)
+        load_scales()
+        load_lib(0)
+        load_lib(1)
+        load_px(2, 1, 0)
+        load_px(2, 1, 1)
+        load_px(3, 2, 0)
+        load_px(3, 2, 1)
+
+        rv32 = keep.tile([PARTS, GROUPS * 4], F32, name="rv32")
+        nc.vector.tensor_copy(out=rv32[:], in_=rv16[:].rearrange("p g t -> p (g t)"))
+
+        sp_bank, sp_grp, sp_codes, sp_scales = {}, {}, {}, {}
+        for g in range(GROUPS):
+            sp_codes[g] = keep.tile([PARTS, 512], U32, name=f"sp_codes{g}", align_bytes=64)
+            sp_scales[g] = keep.tile([PARTS, 512], U8, name=f"sp_scales{g}", align_bytes=64)
+
+        def spec_transpose(g, h):
+            bank = psum.tile([PARTS, 2, 2, 128], F32, name=f"o{2 * g + h}")
+            words = sp_raw[g, h][:].rearrange("m t k -> m (t k)").bitcast(F32)
+            for tt in range(2):
+                for u in range(2):
+                    nc.tensor.transpose(
+                        bank[:, tt, u, :], words[:, 256 * tt + u : 256 * (tt + 1) : 2], ident[:]
+                    )
+            sp_bank[g, h] = bank
+
+        def spec_copy(g, h, on_v=False):
+            grp = keep.tile([PARTS, 1024], BF16, name=f"sp_grp{g}{h}", align_bytes=64)
+            dst = grp[:].bitcast(F32).rearrange("p (t m u) -> p t m u", t=2, u=2)
+            src = sp_bank[g, h][:].rearrange("p t u m -> p t m u")
+            if on_v:
+                nc.vector.tensor_copy(out=dst, in_=src)
+            else:
+                nc.scalar.copy(out=dst, in_=src)
+            sp_grp[g, h] = grp
+
+        def spec_quant(g, h):
+            cols = slice(256 * h, 256 * (h + 1))
+            nc.vector.quantize_mx(
+                out=sp_codes[g][:, cols].bitcast(FP8X4), scales=sp_scales[g][:, cols], in_=sp_grp[g, h][:]
+            )
+
+        ab_grp, ab_codes, ab_scales = {}, {}, {}
+
+        def ab_interleave(i):
+            ab_grp[i] = work.tile([PARTS, WIDTHS[i], 4], BF16, name="ab_grp", align_bytes=64)
+            nc.vector.tensor_copy(
+                out=ab_grp[i][:].rearrange("p (c i) t -> p c t i", i=4),
+                in_=ab_raw[i].rearrange("p t (c i) -> p c t i", i=4),
+            )
+
+        def ab_quant(i):
+            ab_codes[i] = keep.tile([PARTS, WIDTHS[i]], U32, name=f"ab_codes{i}", align_bytes=64)
+            ab_scales[i] = keep.tile([PARTS, WIDTHS[i]], U8, name=f"ab_scales{i}", align_bytes=64)
+            nc.vector.quantize_mx(
+                out=ab_codes[i][:].bitcast(FP8X4),
+                scales=ab_scales[i][:],
+                in_=ab_grp[i][:].rearrange("p n t -> p (n t)"),
+            )
+
+        m_bank, root, z, z_codes, z_scales = {}, {}, {}, {}, {}
+
+        def mm1(u, t):
+            i, g = divmod(u, GROUPS)
+            bank = psum.tile([PARTS, WMAX], F32, name=f"m{t}")
+            nc.tensor.matmul_mx(
+                out=bank[:, : WIDTHS[i]],
+                lhsT=sp_codes[g][:, 128 * t : 128 * (t + 1)].bitcast(FP8X4),
+                lhsT_scale=sp_scales[g][:, 128 * t : 128 * (t + 1)],
+                rhs=ab_codes[i][:].bitcast(FP8X4),
+                rhs_scale=ab_scales[i][:],
+                start=True,
+                stop=True,
+            )
+            m_bank[u, t] = bank
+
+        def rsqrt(u, t):
+            i, g = divmod(u, GROUPS)
+            if t == 0:
+                root[u] = work.tile([PARTS, 4, WIDTHS[i]], F32, name="root", align_bytes=64, bufs=4)
+            nc.scalar.activation(
+                out=root[u][:, t, :],
+                in_=m_bank[u, t][:, : WIDTHS[i]],
+                func=ACT.Abs_reciprocal_sqrt,
+                bias=rv32[:, 4 * g + t : 4 * g + t + 1],
+            )
+
+        def square(u, lo, hi, on_v=False):
+            part = root[u][:, :, lo:hi]
+            if on_v:
+                nc.vector.tensor_tensor(out=part, in0=part, in1=part, op=ALU.mult)
+            else:
+                nc.scalar.activation(out=part, in_=part, func=ACT.Square)
+
+        def weigh(u, lo, hi):
+            i, g = divmod(u, GROUPS)
+            if lo == 0:
+                z[u] = work.tile([PARTS, WIDTHS[i], 4], BF16, name="z", align_bytes=64)
+            nc.vector.tensor_tensor(
+                out=z[u][:, lo:hi, :].rearrange("p (c i) t -> p c t i", i=4),
+                in0=root[u][:, :, lo:hi].rearrange("p t (c i) -> p c t i", i=4),
+                in1=px[i, g][:, :, lo:hi].rearrange("p t (c i) -> p c t i", i=4),
+                op=ALU.mult,
+            )
+
+        def z_quant(u):
+            w = WIDTHS[u // GROUPS]
+            z_codes[u] = work.tile([PARTS, w], U32, name="z_codes", align_bytes=64, bufs=6)
+            z_scales[u] = work.tile([PARTS, w], U8, name="z_scales", align_bytes=64, bufs=6)
+            nc.vector.quantize_mx(
+                out=z_codes[u][:].bitcast(FP8X4),
+                scales=z_scales[u][:],
+                in_=z[u][:].rearrange("p n t -> p (n t)"),
+            )
+
+        blocks = [(i, r, WMAX // WIDTHS[i]) for i in range(TILES) for r in range(0, R // 128, WMAX // WIDTHS[i])]
+        done = {"mm": 0, "out": 0, "banks": 4}
+        o_bank = {}
+
+        def mm2(b):
+            i, r0, nr = blocks[b]
+            bank = psum.tile([PARTS, nr, WIDTHS[i]], F32, name=bank_name(b))
+            step = WMAX if nr == 1 else 128
+            for k in range(nr):
+                r = r0 + k
+                for n0 in range(0, WIDTHS[i], step):
+                    for g in range(GROUPS):
+                        u = GROUPS * i + g
+                        nc.tensor.matmul_mx(
+                            out=bank[:, k, n0 : n0 + step],
+                            lhsT=lib[g][:, 256 * r : 256 * (r + 1)].bitcast(FP4X4),
+                            lhsT_scale=plane[:, g, 128 * r : 128 * (r + 1)],
+                            rhs=z_codes[u][:, n0 : n0 + step].bitcast(FP8X4),
+                            rhs_scale=z_scales[u][:, n0 : n0 + step],
+                            start=(g == 0),
+                            stop=(g == GROUPS - 1),
+                        )
+            o_bank[b] = bank
+
+        free_banks = [f"o{k}" for k in range(4)]
+        bank_of = {}
+
+        def bank_name(b):
+            bank_of[b] = free_banks.pop(0)
+            return bank_of[b]
+
+        def pump():
+            while done["mm"] < len(blocks) and free_banks and GROUPS * blocks[done["mm"]][0] + 1 in z_codes:
+                mm2(done["mm"])
+                done["mm"] += 1
+
+        def emit(on_scalar):
+            b = done["out"]
+            done["out"] += 1
+            i, r0, nr = blocks[b]
+            res = work.tile([PARTS, nr, WIDTHS[i]], F32, name="res", bufs=12, align_bytes=64)
+            if on_scalar:
+                nc.scalar.copy(out=res[:], in_=o_bank[b][:])
+            else:
+                nc.vector.tensor_copy(out=res[:], in_=o_bank[b][:])
+            dst = out[128 * r0 : 128 * (r0 + nr), STARTS[i] : STARTS[i] + WIDTHS[i]]
+            nc.sync.dma_start(out=dst.rearrange("(k p) n -> p k n", p=128), in_=res[:])
+            free_banks.append(bank_of[b])
+
+        for g, h in ((0, 0), (0, 1), (1, 0), (1, 1)):
+            spec_transpose(g, h)
+            spec_copy(g, h)
+        ab_interleave(0)
+        spec_quant(0, 0)
+        ab_quant(0)
+        spec_quant(0, 1)
+        spec_quant(1, 0)
+        spec_quant(1, 1)
+        ab_interleave(1)
+        ab_quant(1)
+        for t in range(4):
+            mm1(0, t)
+        for t in range(4):
+            rsqrt(0, t)
+            mm1(1, t)
+
+        V_PRE = {2: 1, 3: 1, 4: 1, 5: 1, 6: 1, 7: 1, 8: 1}
+        V_POST = {2: 1, 3: 1, 4: 3, 5: 2, 6: 2, 7: 2, 8: 1}
+        S_OUT = {5: 1, 6: 1, 7: 1, 8: 2, 9: 4}
+        SQ_V = {}
+        AB = {1: 2, 2: 3, 3: 4}
+        SPLIT = ()
+
+        for u in range(UNITS):
+            w = WIDTHS[u // GROUPS]
+            cut = SQ_V.get(u, w)
+            cuts = sorted({0, w, cut} | ({w // 2} if u in SPLIT else set()))
+            halves = list(zip(cuts[:-1], cuts[1:]))
+            for lo, hi in halves:
+                square(u, lo, hi, lo >= cut)
+            if u + 1 < UNITS:
+                for t in range(4):
+                    rsqrt(u + 1, t)
+                    if u + 2 < UNITS:
+                        mm1(u + 2, t)
+                if u + 2 == UNITS:
+                    free_banks.extend(f"m{t}" for t in range(4))
+            for lo, hi in halves:
+                weigh(u, lo, hi)
+            for k in range(V_PRE.get(u, 0)):
+                emit(False)
+                pump()
+            z_quant(u)
+            pump()
+            nv, ns = V_POST.get(u, 0), S_OUT.get(u, 0)
+            while nv or ns:
+                if nv >= ns:
+                    emit(False)
+                    nv -= 1
+                else:
+                    emit(True)
+                    ns -= 1
+                pump()
+            if u in AB:
+                ab_interleave(AB[u])
+                ab_quant(AB[u])
+        n = 0
+        while done["out"] < len(blocks):
+            emit(n % 2 == 1)
+            n += 1
+            pump()

@@ -18,7 +18,7 @@ ALU = mybir.AluOpType
 
 PARTS = 128
 GROUPS = L // 512
-WIDTHS = (256, 512, 512, 512, 256)
+WIDTHS = (512, 512, 512, 256, 256)
 STARTS = tuple(sum(WIDTHS[:i]) for i in range(len(WIDTHS)))
 TILES = len(WIDTHS)
 UNITS = TILES * GROUPS
@@ -56,12 +56,18 @@ def tile_poisson_weighted_library_correlation_s13_kernel(
         warm_out = keep.tile([PARTS, 1], F32, name="warm_out")
         nc.scalar.activation(out=warm_out[:], in_=warm[:], func=ACT.Abs_reciprocal_sqrt)
 
-        sp_raw, ab_raw, px, lib = {}, {}, {}, []
+        sp_raw, ab_raw, px, lib = {}, {}, {}, {}
 
         def load_spec(g, h):
             tl = keep.tile([PARTS, 2, F], BF16, name=f"sp_raw{g}{h}", align_bytes=64)
             nc.sync.dma_start(out=tl[:], in_=spec_v[g, :, 2 * h : 2 * h + 2, :])
-            sp_raw[g, h] = tl
+            sp_raw[g, h] = tl[:]
+
+        def load_spec_pair(g):
+            tl = keep.tile([PARTS, 4, F], BF16, name=f"sp_raw{g}", align_bytes=64)
+            nc.sync.dma_start(out=tl[:], in_=spec_v[g])
+            for h in range(2):
+                sp_raw[g, h] = tl[:, 2 * h : 2 * h + 2, :]
 
         def load_ab(i, n):
             w = sum(WIDTHS[i : i + n])
@@ -89,24 +95,21 @@ def tile_poisson_weighted_library_correlation_s13_kernel(
         def load_lib(g):
             tl = keep.tile([PARTS, 2 * R], U8, name=f"lib{g}", align_bytes=64)
             nc.sync.dma_start(out=tl[:].bitcast(I32), in_=words_v[g])
-            lib.append(tl)
+            lib[g] = tl
 
         load_spec(0, 0)
         load_ab(0, 1)
         load_spec(0, 1)
-        load_spec(1, 0)
-        load_spec(1, 1)
+        load_spec_pair(1)
         load_ab(1, 1)
+        load_ab(2, TILES - 2)
         load_px(0, 2, 0)
         load_px(0, 2, 1)
-        load_ab(2, 3)
         load_scales()
+        load_px(2, TILES - 2, 0)
         load_lib(0)
         load_lib(1)
-        load_px(2, 1, 0)
-        load_px(2, 1, 1)
-        load_px(3, 2, 0)
-        load_px(3, 2, 1)
+        load_px(2, TILES - 2, 1)
 
         rv32 = keep.tile([PARTS, GROUPS * 4], F32, name="rv32")
         nc.vector.tensor_copy(out=rv32[:], in_=rv16[:].rearrange("p g t -> p (g t)"))
@@ -118,7 +121,7 @@ def tile_poisson_weighted_library_correlation_s13_kernel(
 
         def spec_transpose(g, h):
             bank = psum.tile([PARTS, 2, 2, 128], F32, name=f"o{2 * g + h}")
-            words = sp_raw[g, h][:].rearrange("m t k -> m (t k)").bitcast(F32)
+            words = sp_raw[g, h].rearrange("m t k -> m (t k)").bitcast(F32)
             for tt in range(2):
                 for u in range(2):
                     nc.tensor.transpose(
@@ -143,6 +146,7 @@ def tile_poisson_weighted_library_correlation_s13_kernel(
             )
 
         ab_grp, ab_codes, ab_scales = {}, {}, {}
+        last_sbuf = {}
 
         def ab_interleave(i):
             ab_grp[i] = work.tile([PARTS, WIDTHS[i], 4], BF16, name="ab_grp", align_bytes=64)
@@ -150,6 +154,7 @@ def tile_poisson_weighted_library_correlation_s13_kernel(
                 out=ab_grp[i][:].rearrange("p (c i) t -> p c t i", i=4),
                 in_=ab_raw[i].rearrange("p t (c i) -> p c t i", i=4),
             )
+            last_sbuf["x"] = ab_grp[i][:, 0, 0:1]
 
         def ab_quant(i):
             ab_codes[i] = keep.tile([PARTS, WIDTHS[i]], U32, name=f"ab_codes{i}", align_bytes=64)
@@ -159,6 +164,7 @@ def tile_poisson_weighted_library_correlation_s13_kernel(
                 scales=ab_scales[i][:],
                 in_=ab_grp[i][:].rearrange("p n t -> p (n t)"),
             )
+            last_sbuf["x"] = ab_codes[i][:, 0:1]
 
         m_bank, root, z, z_codes, z_scales = {}, {}, {}, {}, {}
 
@@ -179,7 +185,7 @@ def tile_poisson_weighted_library_correlation_s13_kernel(
         def rsqrt(u, t):
             i, g = divmod(u, GROUPS)
             if t == 0:
-                root[u] = work.tile([PARTS, 4, WIDTHS[i]], F32, name="root", align_bytes=64, bufs=4)
+                root[u] = work.tile([PARTS, 4, WIDTHS[i]], F32, name="root", align_bytes=64, bufs=6)
             nc.scalar.activation(
                 out=root[u][:, t, :],
                 in_=m_bank[u, t][:, : WIDTHS[i]],
@@ -187,23 +193,30 @@ def tile_poisson_weighted_library_correlation_s13_kernel(
                 bias=rv32[:, 4 * g + t : 4 * g + t + 1],
             )
 
-        def square(u, lo, hi, on_v=False):
+        def square(u, lo, hi, engine):
             part = root[u][:, :, lo:hi]
-            if on_v:
+            if engine == "v":
                 nc.vector.tensor_tensor(out=part, in0=part, in1=part, op=ALU.mult)
+                last_sbuf["x"] = root[u][:, 0, lo : lo + 1]
+            elif engine == "g":
+                after = last_sbuf["x"]
+                hold = work.tile([PARTS, 1], after.dtype, name="hold", bufs=2)
+                nc.gpsimd.tensor_copy(out=hold[:], in_=after)
+                nc.gpsimd.tensor_tensor(out=part, in0=part, in1=part, op=ALU.mult)
             else:
                 nc.scalar.activation(out=part, in_=part, func=ACT.Square)
 
         def weigh(u, lo, hi):
             i, g = divmod(u, GROUPS)
             if lo == 0:
-                z[u] = work.tile([PARTS, WIDTHS[i], 4], BF16, name="z", align_bytes=64)
+                z[u] = work.tile([PARTS, WIDTHS[i], 4], BF16, name="z", align_bytes=64, bufs=4)
             nc.vector.tensor_tensor(
                 out=z[u][:, lo:hi, :].rearrange("p (c i) t -> p c t i", i=4),
                 in0=root[u][:, :, lo:hi].rearrange("p t (c i) -> p c t i", i=4),
                 in1=px[i, g][:, :, lo:hi].rearrange("p t (c i) -> p c t i", i=4),
                 op=ALU.mult,
             )
+            last_sbuf["x"] = z[u][:, lo, 0:1]
 
         def z_quant(u):
             w = WIDTHS[u // GROUPS]
@@ -214,18 +227,34 @@ def tile_poisson_weighted_library_correlation_s13_kernel(
                 scales=z_scales[u][:],
                 in_=z[u][:].rearrange("p n t -> p (n t)"),
             )
+            last_sbuf["x"] = z_codes[u][:, 0:1]
+
+        def z_quant_half(u, h):
+            w = WIDTHS[-1]
+            cols = slice(h * w // 2, (h + 1) * w // 2)
+            if h == 0:
+                z_codes[u] = work.tile([PARTS, w], U32, name="z_codes", align_bytes=64, bufs=6)
+                z_scales[u] = work.tile([PARTS, w], U8, name="z_scales", align_bytes=64, bufs=6)
+            nc.vector.quantize_mx(
+                out=z_codes[u][:, cols].bitcast(FP8X4),
+                scales=z_scales[u][:, cols],
+                in_=z[u][:, cols, :].rearrange("p n t -> p (n t)"),
+            )
+            last_sbuf["x"] = z_codes[u][:, cols.start : cols.start + 1]
 
         blocks = [(i, r, WMAX // WIDTHS[i]) for i in range(TILES) for r in range(0, R // 128, WMAX // WIDTHS[i])]
         done = {"mm": 0, "out": 0, "banks": 4}
         o_bank = {}
 
-        def mm2(b):
+        def mm2(b, columns=None):
             i, r0, nr = blocks[b]
-            bank = psum.tile([PARTS, nr, WIDTHS[i]], F32, name=bank_name(b))
+            if b not in o_bank:
+                o_bank[b] = psum.tile([PARTS, nr, WIDTHS[i]], F32, name=bank_name(b))
+            bank = o_bank[b]
             step = WMAX if nr == 1 else 128
             for k in range(nr):
                 r = r0 + k
-                for n0 in range(0, WIDTHS[i], step):
+                for n0 in columns or range(0, WIDTHS[i], step):
                     for g in range(GROUPS):
                         u = GROUPS * i + g
                         nc.tensor.matmul_mx(
@@ -237,8 +266,21 @@ def tile_poisson_weighted_library_correlation_s13_kernel(
                             start=(g == 0),
                             stop=(g == GROUPS - 1),
                         )
-            o_bank[b] = bank
 
+        last_blocks = [b for b in range(len(blocks)) if blocks[b][0] == TILES - 1]
+
+        def last_products(h):
+            if h == 0:
+                while done["mm"] < len(blocks) and free_banks:
+                    mm2(done["mm"], (0,))
+                    done["mm"] += 1
+            else:
+                for b in range(last_blocks[0], done["mm"]):
+                    mm2(b, (WIDTHS[-1] // 2,))
+                state["all"] = True
+                pump()
+
+        state = {"u": 0, "t": 0}
         free_banks = [f"o{k}" for k in range(4)]
         bank_of = {}
 
@@ -247,12 +289,13 @@ def tile_poisson_weighted_library_correlation_s13_kernel(
             return bank_of[b]
 
         def pump():
-            while done["mm"] < len(blocks) and free_banks and GROUPS * blocks[done["mm"]][0] + 1 in z_codes:
+            while done["mm"] < (len(blocks) if state.get("all") else last_blocks[0]) and free_banks and GROUPS * blocks[done["mm"]][0] + 1 in z_codes:
                 mm2(done["mm"])
                 done["mm"] += 1
 
         def emit(on_scalar):
             b = done["out"]
+            assert b < last_blocks[0] or state.get("all")
             done["out"] += 1
             i, r0, nr = blocks[b]
             res = work.tile([PARTS, nr, WIDTHS[i]], F32, name="res", bufs=12, align_bytes=64)
@@ -266,63 +309,66 @@ def tile_poisson_weighted_library_correlation_s13_kernel(
 
         for g, h in ((0, 0), (0, 1), (1, 0), (1, 1)):
             spec_transpose(g, h)
-            spec_copy(g, h)
-        ab_interleave(0)
-        spec_quant(0, 0)
-        ab_quant(0)
-        spec_quant(0, 1)
-        spec_quant(1, 0)
-        spec_quant(1, 1)
-        ab_interleave(1)
-        ab_quant(1)
-        for t in range(4):
-            mm1(0, t)
-        for t in range(4):
-            rsqrt(0, t)
-            mm1(1, t)
 
-        V_PRE = {2: 1, 3: 1, 4: 1, 5: 1, 6: 1, 7: 1, 8: 1}
-        V_POST = {2: 1, 3: 1, 4: 3, 5: 2, 6: 2, 7: 2, 8: 1}
-        S_OUT = {5: 1, 6: 1, 7: 1, 8: 2, 9: 4}
-        SQ_V = {}
-        AB = {1: 2, 2: 3, 3: 4}
-        SPLIT = ()
+        seen = set()
 
-        for u in range(UNITS):
-            w = WIDTHS[u // GROUPS]
-            cut = SQ_V.get(u, w)
-            cuts = sorted({0, w, cut} | ({w // 2} if u in SPLIT else set()))
-            halves = list(zip(cuts[:-1], cuts[1:]))
-            for lo, hi in halves:
-                square(u, lo, hi, lo >= cut)
-            if u + 1 < UNITS:
+        def first_product():
+            while state["u"] < UNITS:
+                u, t = state["u"], state["t"]
+                i, g = divmod(u, GROUPS)
+                if i not in ab_codes or f"specq:{g}{t // 2}" not in seen or (u > 0 and f"root:{u - 1}" not in seen):
+                    return
+                mm1(u, t)
+                state["t"] = (t + 1) % 4
+                if t == 3:
+                    state["u"] += 1
+
+        ORDER = """
+            turn:01:s turn:00:s inter:0 abq:0 specq:01 turn:10:s specq:00 inter:1 specq:10 turn:11:s specq:11
+            abq:1 root:0 sq:0.0.1:v root:1 inter:2 sq:1.0.1:s root:2 weigh:0.0.2 abq:2 weigh:0.1.2 weigh:1.0.2
+            root:3 weigh:1.1.2 zq:0 zq:1 inter:3 inter:4 abq:3 abq:4 out:v root:4 sq:2.0.2:s out:v sq:3.0.2:g
+            sq:2.1.2:s sq:3.1.2:s sq:4.1.2:s out:v out:v root:5 out:v weigh:2.0.1 weigh:3.0.1 zq:2 root:6 zq:3
+            out:v out:v out:s sq:4.0.2:s sq:5.0.2:s out:v sq:5.1.2:s sq:6.1.2:g root:7 weigh:4.0.1 weigh:5.0.1
+            out:s sq:6.0.2:s zq:4 out:s zq:5 out:s out:s root:8 out:v out:s weigh:6.0.1 out:s sq:7.0.2:s
+            sq:7.1.2:v zq:6 out:v out:v sq:8.0.2:g out:v weigh:7.0.1 sq:8.1.2:s root:9 zq:7 weigh:8.0.2
+            weigh:8.1.2 sq:9.0.2:v out:s zq:8 weigh:9.0.2 out:s zq:9.0 out:s out:s out:s sq:9.1.2:s out:s
+            weigh:9.1.2 zq:9 out:s out:s out:s out:s out:s out:s out:s
+        """
+        for step in ORDER.split():
+            seen.add(step)
+            op, arg = step.split(":")[:2]
+            on_v = step.split(":")[-1] == "v"
+            if op == "turn":
+                spec_copy(int(arg[0]), int(arg[1]), on_v)
+            elif op == "specq":
+                spec_quant(int(arg[0]), int(arg[1]))
+                first_product()
+            elif op == "inter":
+                ab_interleave(int(arg))
+            elif op == "abq":
+                ab_quant(int(arg))
+                first_product()
+            elif op == "root":
                 for t in range(4):
-                    rsqrt(u + 1, t)
-                    if u + 2 < UNITS:
-                        mm1(u + 2, t)
-                if u + 2 == UNITS:
+                    rsqrt(int(arg), t)
+                first_product()
+                if int(arg) == UNITS - 1:
                     free_banks.extend(f"m{t}" for t in range(4))
-            for lo, hi in halves:
-                weigh(u, lo, hi)
-            for k in range(V_PRE.get(u, 0)):
-                emit(False)
-                pump()
-            z_quant(u)
-            pump()
-            nv, ns = V_POST.get(u, 0), S_OUT.get(u, 0)
-            while nv or ns:
-                if nv >= ns:
-                    emit(False)
-                    nv -= 1
+            elif op in ("sq", "weigh"):
+                u, h, n = (int(x) for x in arg.split("."))
+                w = WIDTHS[u // GROUPS] // n
+                if op == "sq":
+                    square(u, h * w, (h + 1) * w, step[-1])
                 else:
-                    emit(True)
-                    ns -= 1
+                    weigh(u, h * w, (h + 1) * w)
+            elif op == "zq":
+                u = int(arg.split(".")[0])
+                if u < UNITS - 1:
+                    z_quant(u)
+                    pump()
+                else:
+                    z_quant_half(u, 0 if "." in arg else 1)
+                    last_products(0 if "." in arg else 1)
+            else:
+                emit(not on_v)
                 pump()
-            if u in AB:
-                ab_interleave(AB[u])
-                ab_quant(AB[u])
-        n = 0
-        while done["out"] < len(blocks):
-            emit(n % 2 == 1)
-            n += 1
-            pump()

@@ -18,7 +18,7 @@ ALU = mybir.AluOpType
 
 PARTS = 128
 GROUPS = L // 512
-WIDTHS = (512, 512, 512, 256, 256)
+WIDTHS = (256, 512, 512, 512, 256)
 STARTS = tuple(sum(WIDTHS[:i]) for i in range(len(WIDTHS)))
 TILES = len(WIDTHS)
 UNITS = TILES * GROUPS
@@ -98,18 +98,18 @@ def tile_poisson_weighted_library_correlation_s13_kernel(
             lib[g] = tl
 
         load_spec(0, 0)
-        load_ab(0, 1)
         load_spec(0, 1)
+        load_ab(0, 1)
         load_spec_pair(1)
         load_ab(1, 1)
-        load_ab(2, TILES - 2)
         load_px(0, 2, 0)
         load_px(0, 2, 1)
-        load_scales()
-        load_px(2, TILES - 2, 0)
+        load_ab(2, TILES - 2)
         load_lib(0)
+        load_scales()
         load_lib(1)
         load_px(2, TILES - 2, 1)
+        load_px(2, TILES - 2, 0)
 
         rv32 = keep.tile([PARTS, GROUPS * 4], F32, name="rv32")
         nc.vector.tensor_copy(out=rv32[:], in_=rv16[:].rearrange("p g t -> p (g t)"))
@@ -324,15 +324,15 @@ def tile_poisson_weighted_library_correlation_s13_kernel(
                     state["u"] += 1
 
         ORDER = """
-            turn:01:s turn:00:s inter:0 abq:0 specq:01 turn:10:s specq:00 inter:1 specq:10 turn:11:s specq:11
-            abq:1 root:0 sq:0.0.1:v root:1 inter:2 sq:1.0.1:s root:2 weigh:0.0.2 abq:2 weigh:0.1.2 weigh:1.0.2
-            root:3 weigh:1.1.2 zq:0 zq:1 inter:3 inter:4 abq:3 abq:4 out:v root:4 sq:2.0.2:s out:v sq:3.0.2:g
-            sq:2.1.2:s sq:3.1.2:s sq:4.1.2:s out:v out:v root:5 out:v weigh:2.0.1 weigh:3.0.1 zq:2 root:6 zq:3
-            out:v out:v out:s sq:4.0.2:s sq:5.0.2:s out:v sq:5.1.2:s sq:6.1.2:g root:7 weigh:4.0.1 weigh:5.0.1
-            out:s sq:6.0.2:s zq:4 out:s zq:5 out:s out:s root:8 out:v out:s weigh:6.0.1 out:s sq:7.0.2:s
-            sq:7.1.2:v zq:6 out:v out:v sq:8.0.2:g out:v weigh:7.0.1 sq:8.1.2:s root:9 zq:7 weigh:8.0.2
-            weigh:8.1.2 sq:9.0.2:v out:s zq:8 weigh:9.0.2 out:s zq:9.0 out:s out:s out:s sq:9.1.2:s out:s
-            weigh:9.1.2 zq:9 out:s out:s out:s out:s out:s out:s out:s
+            turn:00:s turn:01:s turn:10:s inter:0 specq:00 specq:01 abq:0 turn:11:v specq:10 root:0 inter:1
+            sq:0.0.1:s specq:11 abq:1 root:1 root:2 weigh:0.0.1 sq:1.0.1:v zq:0 weigh:1.0.1 inter:2 zq:1
+            sq:2.0.1:s root:3 abq:2 weigh:2.0.1 sq:3.0.2:g sq:3.1.2:s out:v out:v root:4 out:v out:v root:5
+            sq:4.0.1:s inter:3 sq:5.0.1:s weigh:3.0.1 zq:2 abq:3 zq:3 inter:4 root:6 weigh:4.0.1 abq:4 out:s
+            out:s zq:4 weigh:5.0.1 out:v out:v root:7 out:v sq:6.1.2:g sq:6.0.2:s sq:7.0.1:s out:v out:v zq:5
+            out:s weigh:6.0.1 out:s weigh:7.0.1 root:8 out:s out:s out:s out:s zq:6 out:s zq:7 out:v root:9
+            sq:8.1.4:g sq:8.0.4:s out:v out:v sq:8.2.4:g sq:8.3.4:s sq:9.1.4:v sq:9.3.4:v weigh:8.0.1 sq:9.0.4:s
+            weigh:9.0.2 zq:8 out:s zq:9.0 out:s out:s sq:9.2.4:s out:s weigh:9.1.2 out:s out:s out:s zq:9 out:v
+            out:s out:s out:v
         """
         for step in ORDER.split():
             seen.add(step)

from contextlib import ExitStack

import concourse.mybir as mybir
from concourse.masks import make_identity

L, F, P, R = 1024, 512, 2048, 1024
FLOPS = 2 * L * F * P + 2 * L * R * P

F32 = mybir.dt.float32
BF16 = mybir.dt.bfloat16
U32 = mybir.dt.uint32
I32 = mybir.dt.int32
U8 = mybir.dt.uint8
FP8X4 = mybir.dt.float8_e4m3fn_x4
FP4X4 = mybir.dt.float4_e2m1fn_x4
ACT = mybir.ActivationFunctionType
ALU = mybir.AluOpType

PARTS = 128
GROUPS = L // 512
WIDTHS = (256, 512, 512, 512, 256)
STARTS = tuple(sum(WIDTHS[:i]) for i in range(len(WIDTHS)))
TILES = len(WIDTHS)
UNITS = TILES * GROUPS
WMAX = 512


def tile_poisson_weighted_library_correlation_s13_kernel(
    tc, pixels, spectra, abundance, read_var, lib_words, lib_scales, out
):
    nc = tc.nc
    with ExitStack() as ctx:
        keep = ctx.enter_context(tc.tile_pool(name="keep", bufs=1))
        work = ctx.enter_context(tc.tile_pool(name="work", bufs=3))
        psum = ctx.enter_context(tc.psum_pool(name="psum", bufs=1))
        ctx.enter_context(tc.manual_schedule())

        spec_v = spectra.rearrange("(g m t) k -> g m t k", m=128, t=4)
        ab_v = abundance.rearrange("(p j) n -> p j n", j=4)
        px_v = pixels.rearrange("(g p t) n -> g p t n", p=128, t=4)
        rv_v = read_var.rearrange("(g p t) -> p g t", p=128, t=4)
        words_v = lib_words.bitcast(I32)
        scales_v = lib_scales.bitcast(I32).rearrange("g r n -> r g n")

        warm = keep.tile([PARTS, 1], F32, name="warm")
        nc.vector.memset(warm[:], 1.0)
        ident = keep.tile([PARTS, PARTS], F32, name="ident")
        make_identity(nc, ident[:])
        plane = keep.tile([PARTS, GROUPS, R], U8, name="plane", align_bytes=64)
        plane_words = plane[:].rearrange("p g n -> p (g n)").bitcast(I32)
        nc.vector.memset(plane_words, 0)

        rv16 = keep.tile([PARTS, GROUPS, 4], BF16, name="rv16")
        with nc.allow_non_contiguous_dma(reason="2 KiB vector onto the partitions"):
            nc.scalar.dma_start(out=rv16[:], in_=rv_v)
        warm_out = keep.tile([PARTS, 1], F32, name="warm_out")
        nc.scalar.activation(out=warm_out[:], in_=warm[:], func=ACT.Abs_reciprocal_sqrt)

        sp_raw, ab_raw, px, lib = {}, {}, {}, {}

        def load_spec(g, h):
            tl = keep.tile([PARTS, 2, F], BF16, name=f"sp_raw{g}{h}", align_bytes=64)
            nc.sync.dma_start(out=tl[:], in_=spec_v[g, :, 2 * h : 2 * h + 2, :])
            sp_raw[g, h] = tl[:]

        def load_spec_pair(g):
            tl = keep.tile([PARTS, 4, F], BF16, name=f"sp_raw{g}", align_bytes=64)
            nc.sync.dma_start(out=tl[:], in_=spec_v[g])
            for h in range(2):
                sp_raw[g, h] = tl[:, 2 * h : 2 * h + 2, :]

        def load_ab(i, n):
            w = sum(WIDTHS[i : i + n])
            s = STARTS[i]
            tl = keep.tile([PARTS, 4, w], BF16, name=f"ab_raw{i}", align_bytes=64)
            nc.sync.dma_start(out=tl[:], in_=ab_v[:, :, s : s + w])
            for k in range(i, i + n):
                ab_raw[k] = tl[:, :, STARTS[k] - s : STARTS[k] - s + WIDTHS[k]]

        def load_px(i, n, g):
            w = sum(WIDTHS[i : i + n])
            s = STARTS[i]
            tl = keep.tile([PARTS, 4, w], BF16, name=f"px{i}{g}", align_bytes=64)
            nc.sync.dma_start(out=tl[:], in_=px_v[g, :, :, s : s + w])
            for k in range(i, i + n):
                px[k, g] = tl[:, :, STARTS[k] - s : STARTS[k] - s + WIDTHS[k]]

        def load_scales():
            for q in range(4):
                nc.sync.dma_start(
                    out=plane_words[32 * q : 32 * q + 4, :].rearrange("p (g n) -> p g n", g=GROUPS),
                    in_=scales_v[4 * q : 4 * q + 4],
                )

        def load_lib(g):
            tl = keep.tile([PARTS, 2 * R], U8, name=f"lib{g}", align_bytes=64)
            nc.sync.dma_start(out=tl[:].bitcast(I32), in_=words_v[g])
            lib[g] = tl

        load_spec(0, 0)
        load_spec(0, 1)
        load_ab(0, 1)
        load_spec_pair(1)
        load_ab(1, 1)
        load_px(0, 2, 0)
        load_px(0, 2, 1)
        load_ab(2, TILES - 2)
        load_lib(0)
        load_scales()
        load_lib(1)
        load_px(2, TILES - 2, 1)
        load_px(2, TILES - 2, 0)

        rv32 = keep.tile([PARTS, GROUPS * 4], F32, name="rv32")
        nc.vector.tensor_copy(out=rv32[:], in_=rv16[:].rearrange("p g t -> p (g t)"))

        sp_bank, sp_grp, sp_codes, sp_scales = {}, {}, {}, {}
        for g in range(GROUPS):
            sp_codes[g] = keep.tile([PARTS, 512], U32, name=f"sp_codes{g}", align_bytes=64)
            sp_scales[g] = keep.tile([PARTS, 512], U8, name=f"sp_scales{g}", align_bytes=64)

        def spec_transpose(g, h):
            bank = psum.tile([PARTS, 2, 2, 128], F32, name=f"o{2 * g + h}")
            words = sp_raw[g, h].rearrange("m t k -> m (t k)").bitcast(F32)
            for tt in range(2):
                for u in range(2):
                    nc.tensor.transpose(
                        bank[:, tt, u, :], words[:, 256 * tt + u : 256 * (tt + 1) : 2], ident[:]
                    )
            sp_bank[g, h] = bank

        def spec_copy(g, h, on_v=False):
            grp = keep.tile([PARTS, 1024], BF16, name=f"sp_grp{g}{h}", align_bytes=64)
            dst = grp[:].bitcast(F32).rearrange("p (t m u) -> p t m u", t=2, u=2)
            src = sp_bank[g, h][:].rearrange("p t u m -> p t m u")
            if on_v:
                nc.vector.tensor_copy(out=dst, in_=src)
            else:
                nc.scalar.copy(out=dst, in_=src)
            sp_grp[g, h] = grp

        def spec_quant(g, h):
            cols = slice(256 * h, 256 * (h + 1))
            nc.vector.quantize_mx(
                out=sp_codes[g][:, cols].bitcast(FP8X4), scales=sp_scales[g][:, cols], in_=sp_grp[g, h][:]
            )

        ab_grp, ab_codes, ab_scales = {}, {}, {}
        last_sbuf = {}

        def ab_interleave(i):
            ab_grp[i] = work.tile([PARTS, WIDTHS[i], 4], BF16, name="ab_grp", align_bytes=64)
            nc.vector.tensor_copy(
                out=ab_grp[i][:].rearrange("p (c i) t -> p c t i", i=4),
                in_=ab_raw[i].rearrange("p t (c i) -> p c t i", i=4),
            )
            last_sbuf["x"] = ab_grp[i][:, 0, 0:1]

        def ab_quant(i):
            ab_codes[i] = keep.tile([PARTS, WIDTHS[i]], U32, name=f"ab_codes{i}", align_bytes=64)
            ab_scales[i] = keep.tile([PARTS, WIDTHS[i]], U8, name=f"ab_scales{i}", align_bytes=64)
            nc.vector.quantize_mx(
                out=ab_codes[i][:].bitcast(FP8X4),
                scales=ab_scales[i][:],
                in_=ab_grp[i][:].rearrange("p n t -> p (n t)"),
            )
            last_sbuf["x"] = ab_codes[i][:, 0:1]

        m_bank, root, z, z_codes, z_scales = {}, {}, {}, {}, {}

        def mm1(u, t):
            i, g = divmod(u, GROUPS)
            bank = psum.tile([PARTS, WMAX], F32, name=f"m{t}")
            nc.tensor.matmul_mx(
                out=bank[:, : WIDTHS[i]],
                lhsT=sp_codes[g][:, 128 * t : 128 * (t + 1)].bitcast(FP8X4),
                lhsT_scale=sp_scales[g][:, 128 * t : 128 * (t + 1)],
                rhs=ab_codes[i][:].bitcast(FP8X4),
                rhs_scale=ab_scales[i][:],
                start=True,
                stop=True,
            )
            m_bank[u, t] = bank

        def rsqrt(u, t):
            i, g = divmod(u, GROUPS)
            if t == 0:
                root[u] = work.tile([PARTS, 4, WIDTHS[i]], F32, name="root", align_bytes=64, bufs=6)
            nc.scalar.activation(
                out=root[u][:, t, :],
                in_=m_bank[u, t][:, : WIDTHS[i]],
                func=ACT.Abs_reciprocal_sqrt,
                bias=rv32[:, 4 * g + t : 4 * g + t + 1],
            )

        def square(u, lo, hi, engine):
            part = root[u][:, :, lo:hi]
            if engine == "v":
                nc.vector.tensor_tensor(out=part, in0=part, in1=part, op=ALU.mult)
                last_sbuf["x"] = root[u][:, 0, lo : lo + 1]
            elif engine == "g":
                after = last_sbuf["x"]
                hold = work.tile([PARTS, 1], after.dtype, name="hold", bufs=2)
                nc.gpsimd.tensor_copy(out=hold[:], in_=after)
                nc.gpsimd.tensor_tensor(out=part, in0=part, in1=part, op=ALU.mult)
            else:
                nc.scalar.activation(out=part, in_=part, func=ACT.Square)

        def weigh(u, lo, hi):
            i, g = divmod(u, GROUPS)
            if lo == 0:
                z[u] = work.tile([PARTS, WIDTHS[i], 4], BF16, name="z", align_bytes=64, bufs=4)
            nc.vector.tensor_tensor(
                out=z[u][:, lo:hi, :].rearrange("p (c i) t -> p c t i", i=4),
                in0=root[u][:, :, lo:hi].rearrange("p t (c i) -> p c t i", i=4),
                in1=px[i, g][:, :, lo:hi].rearrange("p t (c i) -> p c t i", i=4),
                op=ALU.mult,
            )
            last_sbuf["x"] = z[u][:, lo, 0:1]

        def z_quant(u):
            w = WIDTHS[u // GROUPS]
            z_codes[u] = work.tile([PARTS, w], U32, name="z_codes", align_bytes=64, bufs=6)
            z_scales[u] = work.tile([PARTS, w], U8, name="z_scales", align_bytes=64, bufs=6)
            nc.vector.quantize_mx(
                out=z_codes[u][:].bitcast(FP8X4),
                scales=z_scales[u][:],
                in_=z[u][:].rearrange("p n t -> p (n t)"),
            )
            last_sbuf["x"] = z_codes[u][:, 0:1]

        def z_quant_half(u, h):
            w = WIDTHS[-1]
            cols = slice(h * w // 2, (h + 1) * w // 2)
            if h == 0:
                z_codes[u] = work.tile([PARTS, w], U32, name="z_codes", align_bytes=64, bufs=6)
                z_scales[u] = work.tile([PARTS, w], U8, name="z_scales", align_bytes=64, bufs=6)
            nc.vector.quantize_mx(
                out=z_codes[u][:, cols].bitcast(FP8X4),
                scales=z_scales[u][:, cols],
                in_=z[u][:, cols, :].rearrange("p n t -> p (n t)"),
            )
            last_sbuf["x"] = z_codes[u][:, cols.start : cols.start + 1]

        blocks = [(i, r, WMAX // WIDTHS[i]) for i in range(TILES) for r in range(0, R // 128, WMAX // WIDTHS[i])]
        done = {"mm": 0, "out": 0, "banks": 4}
        o_bank = {}

        def mm2(b, columns=None):
            i, r0, nr = blocks[b]
            if b not in o_bank:
                o_bank[b] = psum.tile([PARTS, nr, WIDTHS[i]], F32, name=bank_name(b))
            bank = o_bank[b]
            step = WMAX if nr == 1 else 128
            for k in range(nr):
                r = r0 + k
                for n0 in columns or range(0, WIDTHS[i], step):
                    for g in range(GROUPS):
                        u = GROUPS * i + g
                        nc.tensor.matmul_mx(
                            out=bank[:, k, n0 : n0 + step],
                            lhsT=lib[g][:, 256 * r : 256 * (r + 1)].bitcast(FP4X4),
                            lhsT_scale=plane[:, g, 128 * r : 128 * (r + 1)],
                            rhs=z_codes[u][:, n0 : n0 + step].bitcast(FP8X4),
                            rhs_scale=z_scales[u][:, n0 : n0 + step],
                            start=(g == 0),
                            stop=(g == GROUPS - 1),
                        )

        last_blocks = [b for b in range(len(blocks)) if blocks[b][0] == TILES - 1]

        def last_products(h):
            if h == 0:
                while done["mm"] < len(blocks) and free_banks:
                    mm2(done["mm"], (0,))
                    done["mm"] += 1
            else:
                for b in range(last_blocks[0], done["mm"]):
                    mm2(b, (WIDTHS[-1] // 2,))
                state["all"] = True
                pump()

        state = {"u": 0, "t": 0}
        free_banks = [f"o{k}" for k in range(4)]
        bank_of = {}

        def bank_name(b):
            bank_of[b] = free_banks.pop(0)
            return bank_of[b]

        def pump():
            while done["mm"] < (len(blocks) if state.get("all") else last_blocks[0]) and free_banks and GROUPS * blocks[done["mm"]][0] + 1 in z_codes:
                mm2(done["mm"])
                done["mm"] += 1

        def emit(on_scalar):
            b = done["out"]
            assert b < last_blocks[0] or state.get("all")
            done["out"] += 1
            i, r0, nr = blocks[b]
            res = work.tile([PARTS, nr, WIDTHS[i]], F32, name="res", bufs=12, align_bytes=64)
            if on_scalar:
                nc.scalar.copy(out=res[:], in_=o_bank[b][:])
            else:
                nc.vector.tensor_copy(out=res[:], in_=o_bank[b][:])
            dst = out[128 * r0 : 128 * (r0 + nr), STARTS[i] : STARTS[i] + WIDTHS[i]]
            nc.sync.dma_start(out=dst.rearrange("(k p) n -> p k n", p=128), in_=res[:])
            free_banks.append(bank_of[b])

        for g, h in ((0, 0), (0, 1), (1, 0), (1, 1)):
            spec_transpose(g, h)

        seen = set()

        def first_product():
            while state["u"] < UNITS:
                u, t = state["u"], state["t"]
                i, g = divmod(u, GROUPS)
                if i not in ab_codes or f"specq:{g}{t // 2}" not in seen or (u > 0 and f"root:{u - 1}" not in seen):
                    return
                mm1(u, t)
                state["t"] = (t + 1) % 4
                if t == 3:
                    state["u"] += 1

        ORDER = """
            turn:00:s turn:01:s turn:10:s inter:0 specq:00 specq:01 abq:0 turn:11:v specq:10 root:0 inter:1
            sq:0.0.1:s specq:11 abq:1 root:1 root:2 weigh:0.0.1 sq:1.0.1:v zq:0 weigh:1.0.1 inter:2 zq:1
            sq:2.0.1:s root:3 abq:2 weigh:2.0.1 sq:3.0.2:g sq:3.1.2:s out:v out:v root:4 out:v out:v root:5
            sq:4.0.1:s inter:3 sq:5.0.1:s weigh:3.0.1 zq:2 abq:3 zq:3 inter:4 root:6 weigh:4.0.1 abq:4 out:s
            out:s zq:4 weigh:5.0.1 out:v out:v root:7 out:v sq:6.1.2:g sq:6.0.2:s sq:7.0.1:s out:v out:v zq:5
            out:s weigh:6.0.1 out:s weigh:7.0.1 root:8 out:s out:s out:s out:s zq:6 out:s zq:7 out:v root:9
            sq:8.1.4:g sq:8.0.4:s out:v out:v sq:8.2.4:g sq:8.3.4:s sq:9.1.4:v sq:9.3.4:v weigh:8.0.1 sq:9.0.4:s
            weigh:9.0.2 zq:8 out:s zq:9.0 out:s out:s sq:9.2.4:s out:s weigh:9.1.2 out:s out:s out:s zq:9 out:v
            out:s out:s out:v
        """
        for step in ORDER.split():
            seen.add(step)
            op, arg = step.split(":")[:2]
            on_v = step.split(":")[-1] == "v"
            if op == "turn":
                spec_copy(int(arg[0]), int(arg[1]), on_v)
            elif op == "specq":
                spec_quant(int(arg[0]), int(arg[1]))
                first_product()
            elif op == "inter":
                ab_interleave(int(arg))
            elif op == "abq":
                ab_quant(int(arg))
                first_product()
            elif op == "root":
                for t in range(4):
                    rsqrt(int(arg), t)
                first_product()
                if int(arg) == UNITS - 1:
                    free_banks.extend(f"m{t}" for t in range(4))
            elif op in ("sq", "weigh"):
                u, h, n = (int(x) for x in arg.split("."))
                w = WIDTHS[u // GROUPS] // n
                if op == "sq":
                    square(u, h * w, (h + 1) * w, step[-1])
                else:
                    weigh(u, h * w, (h + 1) * w)
            elif op == "zq":
                u = int(arg.split(".")[0])
                if u < UNITS - 1:
                    z_quant(u)
                    pump()
                else:
                    z_quant_half(u, 0 if "." in arg else 1)
                    last_products(0 if "." in arg else 1)
            else:
                emit(not on_v)
                pump()
